import numpy as np
import ml_dtypes


def mxq(x, axis, fmt="e4m3"):
    dtype, down = {"e4m3": (ml_dtypes.float8_e4m3fn, 7), "e5m2": (ml_dtypes.float8_e5m2, 14)}[fmt]
    v = np.moveaxis(np.asarray(x, np.float32).astype(ml_dtypes.bfloat16).astype(np.float64), axis, -1)
    blocks = v.reshape(v.shape[:-1] + (-1, 32))
    amax = np.abs(blocks).max(-1, keepdims=True)
    byte = np.maximum(np.where(amax > 0, np.frexp(amax)[1] - 1 + 127, 0) - down, 1)
    scale = np.exp2(byte - 127.0)
    codes = (blocks / scale).astype(np.float32).astype(dtype).astype(np.float64)
    return np.moveaxis((codes * scale).reshape(v.shape), -1, axis)


WIDE = False


def mx_kscale(k, group=512):
    if not WIDE:
        return np.ones(k)
    levels = np.array([18, -18])
    if group != 512:
        return np.exp2(np.random.permutation(np.resize(levels, k // group))).repeat(group)
    if k % 512:
        return np.exp2(np.random.permutation(np.resize(levels, k // 32))).repeat(32)
    a = np.empty((k // 512, 16))
    for p in range(k // 512):
        a[p, :8] = np.random.permutation(np.resize(levels, 8))
        for g in range(8):
            far = levels[np.abs(levels - a[p, g]) >= 10]
            a[p, g + 8] = far[np.random.randint(len(far))]
    return np.exp2(a.ravel()).repeat(32)


def f64(x):
    return np.asarray(x).astype(np.float64)


G, D, I, N, J = 4, 128, 128, 512, 128


def sgn(shape):
    return np.random.uniform(0.5, 2.0, shape) * np.where(np.random.standard_normal(shape) < 0, -1.0, 1.0)


def setup_inputs():
    n = np.random.standard_normal
    s_d = mx_kscale(D, 0)
    s_i = mx_kscale(I, 0)
    return {
        "x": (n((G, D, I)) * s_d[:, None]).astype(np.float32),
        "w": (n((D, N)) / np.sqrt(D) / s_d[:, None]).astype(np.float32),
        "ni": (sgn((G, I, 1)) * s_i[:, None]).astype(np.float32),
        "ad": ((np.random.uniform(size=(G, I, J)) < 0.1) * np.random.uniform(0.5, 1.0, (G, I, J)) / 3 / s_i[:, None]).astype(np.float32),
        "wo": (n((D, N)) / np.sqrt(D) / s_d[:, None]).astype(np.float32),
        "nj": (np.random.uniform(0.5, 2.0, (G, J, 1))).astype(np.float32),
    }


def reference(x, w, ni, ad, wo, nj):
    xq = mxq(f64(x), 1, "e4m3")
    wq = mxq(f64(w), 0, "e4m3")
    z = xq.transpose(0, 2, 1) @ wq
    h = z * f64(ni)
    adq = mxq(f64(ad), 1, "e4m3")
    hq = mxq(h, 1, "e4m3")
    y = adq.transpose(0, 2, 1) @ hq
    woq = mxq(f64(wo), 0, "e4m3")
    o = xq.transpose(0, 2, 1) @ woq
    out_ = np.maximum(y * f64(nj) + o, 0.0)
    return out_

@@ -1,0 +1,169 @@
+from contextlib import ExitStack
+
+import concourse.mybir as mybir
+
+G, D, I, N, J = 4, 128, 128, 512, 128
+FLOPS = 3 * 2 * G * 128 * 128 * N
+
+F32 = mybir.dt.float32
+BF16 = mybir.dt.bfloat16
+I32 = mybir.dt.int32
+U8 = mybir.dt.uint8
+FP8X4 = mybir.dt.float8_e4m3fn_x4
+ACT = mybir.ActivationFunctionType
+ALU = mybir.AluOpType
+
+P = 128
+R = 32
+PACK = 4
+HALF = N // 2
+NT = 128
+SCALE_WORDS = HALF // 4
+
+
+def tile_rows_gnn_sage_kernel(tc, x, w, ni, ad, wo, nj, out):
+    nc = tc.nc
+    with ExitStack() as ctx:
+        sb = ctx.enter_context(tc.tile_pool(name="sb", bufs=1))
+        ps = ctx.enter_context(tc.psum_pool(name="ps", bufs=1))
+        ctx.enter_context(tc.manual_schedule())
+
+        def tile(name, shape, dtype):
+            return sb.tile(shape, dtype, name=name, align_bytes=64)
+
+        def rows(g):
+            return slice(R * g, R * (g + 1))
+
+        def cols(g, phase):
+            half = (g // 2) ^ phase
+            return slice(HALF * half, HALF * (half + 1))
+
+        banks = [[ps.tile([P, 512], F32, name=f"bank{ph}_{g}") for g in range(G)] for ph in range(2)]
+
+        x_raw = tile("x_raw", [P, PACK, I], F32)
+        ad_raw = tile("ad_raw", [P, PACK, J], F32)
+        w_raw = tile("w_raw", [P, PACK, HALF], F32)
+        wo_raw = tile("wo_raw", [P, PACK, HALF], F32)
+        node_rows = tile("node_rows", [P, G * R], F32)
+        node_cols = tile("node_cols", [P, G * R], F32)
+        x_b = tile("x_b", [P, I, PACK], BF16)
+        ad_b = tile("ad_b", [P, J, PACK], BF16)
+        w_b = tile("w_b", [P, HALF, PACK], BF16)
+        wo_b = tile("wo_b", [P, HALF, PACK], BF16)
+        x_c = tile("x_c", [P, I], I32)
+        x_s = tile("x_s", [P, I], U8)
+        ad_c = tile("ad_c", [P, J], I32)
+        ad_s = tile("ad_s", [P, J], U8)
+        w_q = [tile(f"w_q{ph}", [P, HALF + SCALE_WORDS], I32) for ph in range(2)]
+        wo_q = [tile(f"wo_q{ph}", [P, HALF + SCALE_WORDS], I32) for ph in range(2)]
+        h_nodes = [[tile(f"h_nodes{ph}_{g}", [P, HALF], BF16) for g in range(G)] for ph in range(2)]
+        h_rows = [tile(f"h_rows{ph}", [P, PACK, HALF], BF16) for ph in range(2)]
+        h_b = [tile(f"h_b{ph}", [P, HALF, PACK], BF16) for ph in range(2)]
+        h_c = [tile(f"h_c{ph}", [P, HALF], I32) for ph in range(2)]
+        h_s = [tile(f"h_s{ph}", [P, HALF], U8) for ph in range(2)]
+        o_sb = [[tile(f"o_sb{ph}_{g}", [P, HALF], F32) for g in range(G)] for ph in range(2)]
+        pre = [[tile(f"pre{ph}_{g}", [P, HALF], F32) for g in range(G)] for ph in range(2)]
+        res = [[tile(f"res{ph}_{g}", [P, HALF], F32) for g in range(G)] for ph in range(2)]
+
+        def load_half(dst, src):
+            for g in (0, 2, 1, 3):
+                nc.sync.dma_start(out=dst[rows(g)], in_=src[:, cols(g, 0)].rearrange("(p j) n -> p j n", j=PACK))
+
+        def interleave(engine_copy, dst, src, c0, c1):
+            engine_copy(out=dst[:, c0:c1, :], in_=src[:, :, c0:c1].rearrange("p j n -> p n j"))
+
+        def quantize(codes, scales, src):
+            nc.vector.quantize_mx(out=codes.bitcast(FP8X4), scales=scales, in_=src[:].rearrange("p n j -> p (n j)"))
+
+        def codes_of(q):
+            return q[:, 0:HALF]
+
+        def scales_of(q):
+            return q[:, HALF:HALF + SCALE_WORDS].bitcast(U8)
+
+        def swap(q):
+            nc.sync.dma_start(out=q[1][0:64, :], in_=q[0][64:128, :])
+            nc.sync.dma_start(out=q[1][64:128, :], in_=q[0][0:64, :])
+
+        def product(ph, lhs_c, lhs_s, rhs_c, rhs_s):
+            for c in range(HALF // NT):
+                n = slice(NT * c, NT * (c + 1))
+                for g in range(G):
+                    nc.tensor.matmul_mx(
+                        out=banks[ph][g][:, n],
+                        lhsT=lhs_c[rows(g), :].bitcast(FP8X4),
+                        lhsT_scale=lhs_s[rows(g), :],
+                        rhs=rhs_c[rows(g), n].bitcast(FP8X4),
+                        rhs_scale=rhs_s[rows(g), n],
+                        start=True,
+                        stop=True,
+                    )
+
+        def scale_z(ph):
+            for g in (0, 2, 1, 3):
+                if g < 2:
+                    nc.scalar.activation(out=h_nodes[ph][g][:], in_=banks[ph][g][:, 0:HALF], func=ACT.Copy, scale=node_cols[:, R * g : R * g + 1])
+                else:
+                    nc.vector.tensor_scalar(out=h_nodes[ph][g][:], in0=banks[ph][g][:, 0:HALF], scalar1=node_cols[:, R * g : R * g + 1], scalar2=None, op0=ALU.mult)
+                nc.sync.dma_start(out=h_rows[ph][rows(g)], in_=h_nodes[ph][g][:])
+
+        def copy_o(ph):
+            for g in range(G):
+                nc.scalar.copy(out=o_sb[ph][g][:], in_=banks[ph][g][:, 0:HALF])
+
+        def combine(ph, g):
+            nc.vector.scalar_tensor_tensor(out=pre[ph][g][:], in0=banks[ph][g][:, 0:HALF], scalar=node_cols[:, R * g + 1 : R * g + 2], in1=o_sb[ph][g][:], op0=ALU.mult, op1=ALU.add)
+
+        def finish(ph, g):
+            nc.scalar.activation(out=res[ph][g][:], in_=pre[ph][g][:], func=ACT.Relu)
+            nc.sync.dma_start(out=out[g, :, cols(g, ph)], in_=res[ph][g][:])
+
+        nc.sync.dma_start(out=x_raw[:], in_=x.rearrange("g (p j) i -> (g p) j i", j=PACK))
+        load_half(w_raw, w)
+        load_half(wo_raw, wo)
+        nc.sync.dma_start(out=ad_raw[:], in_=ad.rearrange("g (p j) c -> (g p) j c", j=PACK))
+        nc.gpsimd.memset(node_rows[:], 0.0)
+        for place, factor in enumerate((ni, nj)):
+            nc.gpsimd.dma_start(
+                out=node_rows[place:P:R, :].rearrange("q (g a) -> q g a", a=R),
+                in_=factor.rearrange("g (q a) o -> q g (a o)", a=R),
+            )
+        nc.vector.memset(w_q[0][:, HALF:], 0)
+        nc.vector.memset(wo_q[0][:, HALF:], 0)
+
+        interleave(nc.scalar.copy, x_b, x_raw, 0, I)
+        interleave(nc.vector.tensor_copy, w_b, w_raw, 0, HALF)
+        quantize(x_c[:], x_s[:], x_b)
+        quantize(codes_of(w_q[0]), scales_of(w_q[0]), w_b)
+        swap(w_q)
+        nc.vector.transpose(out=node_cols[:], in_=node_rows[:])
+        product(0, x_c, x_s, codes_of(w_q[0]), scales_of(w_q[0]))
+        scale_z(0)
+
+        interleave(nc.vector.tensor_copy, wo_b, wo_raw, 0, HALF)
+        interleave(nc.scalar.copy, ad_b, ad_raw, 0, J)
+        quantize(ad_c[:], ad_s[:], ad_b)
+        quantize(codes_of(wo_q[0]), scales_of(wo_q[0]), wo_b)
+        product(1, x_c, x_s, codes_of(w_q[1]), scales_of(w_q[1]))
+        swap(wo_q)
+        product(0, x_c, x_s, codes_of(wo_q[0]), scales_of(wo_q[0]))
+        scale_z(1)
+        copy_o(0)
+
+        interleave(nc.vector.tensor_copy, h_b[0], h_rows[0], 0, HALF)
+        quantize(h_c[0][:], h_s[0][:], h_b[0])
+        product(1, x_c, x_s, codes_of(wo_q[1]), scales_of(wo_q[1]))
+        product(0, ad_c, ad_s, h_c[0], h_s[0])
+        copy_o(1)
+        combine(0, 0)
+        combine(0, 1)
+        interleave(nc.vector.tensor_copy, h_b[1], h_rows[1], 0, HALF)
+        combine(0, 2)
+        quantize(h_c[1][:], h_s[1][:], h_b[1])
+        product(1, ad_c, ad_s, h_c[1], h_s[1])
+        combine(0, 3)
+        for g in range(G):
+            finish(0, g)
+        for g in range(G):
+            combine(1, g)
+            finish(1, g)

@@ -15,10 +15,10 @@ ALU = mybir.AluOpType
 
 P = 128
 R = 32
+TILES = P // R
 PACK = 4
-HALF = N // 2
-NT = 128
-SCALE_WORDS = HALF // 4
+RUN = 8
+NT = N // TILES
 
 
 def tile_rows_gnn_sage_kernel(tc, x, w, ni, ad, wo, nj, out):
@@ -31,139 +31,176 @@ def tile_rows_gnn_sage_kernel(tc, x, w, ni, ad, wo, nj, out):
         def tile(name, shape, dtype):
             return sb.tile(shape, dtype, name=name, align_bytes=64)
 
-        def rows(g):
-            return slice(R * g, R * (g + 1))
+        def rows(r):
+            return slice(R * r, R * (r + 1))
 
-        def cols(g, phase):
-            half = (g // 2) ^ phase
-            return slice(HALF * half, HALF * (half + 1))
+        def block(c):
+            return slice(NT * c, NT * (c + 1))
 
-        banks = [[ps.tile([P, 512], F32, name=f"bank{ph}_{g}") for g in range(G)] for ph in range(2)]
+        zy_bank = [ps.tile([P, 512], F32, name=f"zy_bank{r}") for r in range(TILES)]
+        o_bank = [ps.tile([P, 512], F32, name=f"o_bank{r}") for r in range(TILES)]
 
-        x_raw = tile("x_raw", [P, PACK, I], F32)
+        x_raw = tile("x_raw", [P, G, PACK, I], F32)
         ad_raw = tile("ad_raw", [P, PACK, J], F32)
-        w_raw = tile("w_raw", [P, PACK, HALF], F32)
-        wo_raw = tile("wo_raw", [P, PACK, HALF], F32)
-        node_rows = tile("node_rows", [P, G * R], F32)
-        node_cols = tile("node_cols", [P, G * R], F32)
-        x_b = tile("x_b", [P, I, PACK], BF16)
+        w_raw = tile("w_raw", [P, PACK, NT], F32)
+        wo_raw = tile("wo_raw", [P, PACK, NT], F32)
+        ni_row = tile("ni_row", [P, I], F32)
+        ni_dealt = tile("ni_dealt", [P, I], F32)
+        ni_cols = tile("ni_cols", [P, I], F32)
+        nj_rows = tile("nj_rows", [P, J], F32)
+        nj_cols = tile("nj_cols", [P, J], F32)
+        ni_t = tile("ni_t", [P, PACK], F32)
+        x_b = tile("x_b", [P, PACK, G * R * PACK], BF16)
         ad_b = tile("ad_b", [P, J, PACK], BF16)
-        w_b = tile("w_b", [P, HALF, PACK], BF16)
-        wo_b = tile("wo_b", [P, HALF, PACK], BF16)
-        x_c = tile("x_c", [P, I], I32)
-        x_s = tile("x_s", [P, I], U8)
+        w_b = tile("w_b", [P, NT, PACK], BF16)
+        wo_b = tile("wo_b", [P, NT, PACK], BF16)
+        xz_c = tile("xz_c", [P, G * I], I32)
+        xz_s = tile("xz_s", [P, G * I], U8)
+        xo_c = tile("xo_c", [P, G * I], I32)
+        xo_s = tile("xo_s", [P, G * I], U8)
+        w_c = tile("w_c", [P, NT], I32)
+        w_s = tile("w_s", [P, NT], U8)
+        wo_c = tile("wo_c", [P, NT], I32)
+        wo_s = tile("wo_s", [P, NT], U8)
         ad_c = tile("ad_c", [P, J], I32)
         ad_s = tile("ad_s", [P, J], U8)
-        w_q = [tile(f"w_q{ph}", [P, HALF + SCALE_WORDS], I32) for ph in range(2)]
-        wo_q = [tile(f"wo_q{ph}", [P, HALF + SCALE_WORDS], I32) for ph in range(2)]
-        h_nodes = [[tile(f"h_nodes{ph}_{g}", [P, HALF], BF16) for g in range(G)] for ph in range(2)]
-        h_rows = [tile(f"h_rows{ph}", [P, PACK, HALF], BF16) for ph in range(2)]
-        h_b = [tile(f"h_b{ph}", [P, HALF, PACK], BF16) for ph in range(2)]
-        h_c = [tile(f"h_c{ph}", [P, HALF], I32) for ph in range(2)]
-        h_s = [tile(f"h_s{ph}", [P, HALF], U8) for ph in range(2)]
-        o_sb = [[tile(f"o_sb{ph}_{g}", [P, HALF], F32) for g in range(G)] for ph in range(2)]
-        pre = [[tile(f"pre{ph}_{g}", [P, HALF], F32) for g in range(G)] for ph in range(2)]
-        res = [[tile(f"res{ph}_{g}", [P, HALF], F32) for g in range(G)] for ph in range(2)]
+        h_b = [tile(f"h_b{c}", [P, NT, PACK], BF16) for c in range(TILES)]
+        h_c = [tile(f"h_c{c}", [P, NT], I32) for c in range(TILES)]
+        h_s = [tile(f"h_s{c}", [P, NT], U8) for c in range(TILES)]
+        o_sb = tile("o_sb", [P, TILES, G, NT], F32)
+        pre = [tile(f"pre{g}", [P, N], F32) for g in range(G)]
+        res = [tile(f"res{g}", [P, N], F32) for g in range(G)]
 
-        def load_half(dst, src):
-            for g in (0, 2, 1, 3):
-                nc.sync.dma_start(out=dst[rows(g)], in_=src[:, cols(g, 0)].rearrange("(p j) n -> p j n", j=PACK))
+        load_order = (0, 2, 1, 3)
 
-        def interleave(engine_copy, dst, src, c0, c1):
-            engine_copy(out=dst[:, c0:c1, :], in_=src[:, :, c0:c1].rearrange("p j n -> p n j"))
+        def load_columns(dst, src):
+            for r in load_order:
+                nc.sync.dma_start(out=dst[rows(r)], in_=src[:, block(r)].rearrange("(p j) n -> p j n", j=PACK))
+
+        def interleave(engine_copy, dst, src):
+            engine_copy(out=dst[:], in_=src[:].rearrange("p j n -> p n j"))
+
+        def deal_x(engine_copy, t, g0, g1):
+            engine_copy(
+                out=x_b[:, t, g0 * R * PACK : g1 * R * PACK].rearrange("p (g b q j) -> p g b q j", b=4, q=RUN, j=PACK),
+                in_=x_raw[:, g0:g1].rearrange("p g j (b t q) -> p t g b q j", t=PACK, q=RUN)[:, t],
+            )
 
         def quantize(codes, scales, src):
-            nc.vector.quantize_mx(out=codes.bitcast(FP8X4), scales=scales, in_=src[:].rearrange("p n j -> p (n j)"))
+            nc.vector.quantize_mx(out=codes.bitcast(FP8X4), scales=scales, in_=src)
 
-        def codes_of(q):
-            return q[:, 0:HALF]
+        def flat(t):
+            return t[:].rearrange("p n j -> p (n j)")
 
-        def scales_of(q):
-            return q[:, HALF:HALF + SCALE_WORDS].bitcast(U8)
-
-        def swap(q):
-            nc.sync.dma_start(out=q[1][0:64, :], in_=q[0][64:128, :])
-            nc.sync.dma_start(out=q[1][64:128, :], in_=q[0][0:64, :])
-
-        def product(ph, lhs_c, lhs_s, rhs_c, rhs_s):
-            for c in range(HALF // NT):
-                n = slice(NT * c, NT * (c + 1))
-                for g in range(G):
-                    nc.tensor.matmul_mx(
-                        out=banks[ph][g][:, n],
-                        lhsT=lhs_c[rows(g), :].bitcast(FP8X4),
-                        lhsT_scale=lhs_s[rows(g), :],
-                        rhs=rhs_c[rows(g), n].bitcast(FP8X4),
-                        rhs_scale=rhs_s[rows(g), n],
-                        start=True,
-                        stop=True,
-                    )
-
-        def scale_z(ph):
-            for g in (0, 2, 1, 3):
-                if g < 2:
-                    nc.scalar.activation(out=h_nodes[ph][g][:], in_=banks[ph][g][:, 0:HALF], func=ACT.Copy, scale=node_cols[:, R * g : R * g + 1])
-                else:
-                    nc.vector.tensor_scalar(out=h_nodes[ph][g][:], in0=banks[ph][g][:, 0:HALF], scalar1=node_cols[:, R * g : R * g + 1], scalar2=None, op0=ALU.mult)
-                nc.sync.dma_start(out=h_rows[ph][rows(g)], in_=h_nodes[ph][g][:])
-
-        def copy_o(ph):
-            for g in range(G):
-                nc.scalar.copy(out=o_sb[ph][g][:], in_=banks[ph][g][:, 0:HALF])
-
-        def combine(ph, g):
-            nc.vector.scalar_tensor_tensor(out=pre[ph][g][:], in0=banks[ph][g][:, 0:HALF], scalar=node_cols[:, R * g + 1 : R * g + 2], in1=o_sb[ph][g][:], op0=ALU.mult, op1=ALU.add)
-
-        def finish(ph, g):
-            nc.scalar.activation(out=res[ph][g][:], in_=pre[ph][g][:], func=ACT.Relu)
-            nc.sync.dma_start(out=out[g, :, cols(g, ph)], in_=res[ph][g][:])
-
-        nc.sync.dma_start(out=x_raw[:], in_=x.rearrange("g (p j) i -> (g p) j i", j=PACK))
-        load_half(w_raw, w)
-        load_half(wo_raw, wo)
-        nc.sync.dma_start(out=ad_raw[:], in_=ad.rearrange("g (p j) c -> (g p) j c", j=PACK))
-        nc.gpsimd.memset(node_rows[:], 0.0)
-        for place, factor in enumerate((ni, nj)):
-            nc.gpsimd.dma_start(
-                out=node_rows[place:P:R, :].rearrange("q (g a) -> q g a", a=R),
-                in_=factor.rearrange("g (q a) o -> q g (a o)", a=R),
+        def product(dst, r, lhs_c, lhs_s, m, rhs_c, rhs_s):
+            nc.tensor.matmul_mx(
+                out=dst,
+                lhsT=lhs_c[rows(r), m].bitcast(FP8X4),
+                lhsT_scale=lhs_s[rows(r), m],
+                rhs=rhs_c[rows(r), :].bitcast(FP8X4),
+                rhs_scale=rhs_s[rows(r), :],
+                start=True,
+                stop=True,
             )
-        nc.vector.memset(w_q[0][:, HALF:], 0)
-        nc.vector.memset(wo_q[0][:, HALF:], 0)
 
-        interleave(nc.scalar.copy, x_b, x_raw, 0, I)
-        interleave(nc.vector.tensor_copy, w_b, w_raw, 0, HALF)
-        quantize(x_c[:], x_s[:], x_b)
-        quantize(codes_of(w_q[0]), scales_of(w_q[0]), w_b)
-        swap(w_q)
-        nc.vector.transpose(out=node_cols[:], in_=node_rows[:])
-        product(0, x_c, x_s, codes_of(w_q[0]), scales_of(w_q[0]))
+        def scale_z(c):
+            nc.vector.tensor_tensor(
+                out=h_b[c][:],
+                in0=zy_bank[c][:].rearrange("p (t n) -> p n t", t=PACK),
+                in1=ni_t[:].unsqueeze(1).to_broadcast([P, NT, PACK]),
+                op=ALU.mult,
+            )
+
+        def quantize_h(c):
+            quantize(h_c[c][:], h_s[c][:], flat(h_b[c]))
+
+        def edges(g, c):
+            product(zy_bank[g][:, block(c)], g, ad_c, ad_s, slice(0, J), h_c[c], h_s[c])
+
+        nc.gpsimd.memset(ni_row[:], 0.0)
+        nc.scalar.dma_start(out=ni_row[0:P:R, :], in_=ni.rearrange("g i o -> g (i o)"))
+        load_columns(w_raw, w)
+        for r in load_order:
+            nc.sync.dma_start(
+                out=x_raw[rows(r)].rearrange("p g j i -> p g (j i)"),
+                in_=x.rearrange("g (p j) i -> p g (j i)", j=PACK),
+            )
+        load_columns(wo_raw, wo)
+        ad_dealt = ad.rearrange("g (b t q) c -> t (g b) q c", t=PACK, q=RUN)
+        for t in range(PACK):
+            nc.sync.dma_start(out=ad_raw[:, t, :], in_=ad_dealt[t])
+
+        nc.gpsimd.memset(nj_rows[:], 0.0)
+        nc.gpsimd.dma_start(
+            out=nj_rows[0:P:R, :].rearrange("q (g a) -> q g a", a=R),
+            in_=nj.rearrange("g (q a) o -> q g (a o)", a=R),
+        )
+        nc.vector.memset(xz_s[:].bitcast(I32), 0)
+
+        interleave(nc.scalar.copy, w_b, w_raw)
+        nc.vector.tensor_copy(
+            out=ni_dealt[:].rearrange("p (t b q) -> p t b q", t=PACK, q=RUN),
+            in_=ni_row[:].rearrange("p (b t q) -> p t b q", t=PACK, q=RUN),
+        )
+        nc.vector.transpose(out=ni_cols[:], in_=ni_dealt[:])
+        nc.vector.tensor_copy(out=ni_t[:], in_=ni_cols[:, 0:P:R])
+        quantize(w_c[:], w_s[:], flat(w_b))
+
+        deal_x(nc.vector.tensor_copy, 0, 0, G)
+        deal_x(nc.scalar.copy, 1, 0, G)
+        deal_x(nc.vector.tensor_copy, 2, 0, G)
+        deal_x(nc.scalar.copy, 3, 2, G)
+        deal_x(nc.vector.tensor_copy, 3, 0, 2)
+        for u in range(2):
+            half = slice(2 * P * u, 2 * P * (u + 1))
+            quantize(xz_c[:, half], xz_s[:, half], x_b[:, 2 * u : 2 * u + 2, :].rearrange("p t e -> p (t e)"))
+        for r in range(TILES):
+            for t in range(PACK):
+                product(zy_bank[r][:, block(t)], r, xz_c, xz_s, block(t), w_c, w_s)
+
+        interleave(nc.scalar.copy, wo_b, wo_raw)
+        interleave(nc.scalar.copy, ad_b, ad_raw)
+        quantize(wo_c[:], wo_s[:], flat(wo_b))
+        nc.vector.tensor_copy(
+            out=xo_c[:].rearrange("p (a t q) -> p a t q", t=PACK, q=RUN),
+            in_=xz_c[:].rearrange("p (t a q) -> p a t q", t=PACK, q=RUN),
+        )
+        nc.vector.tensor_copy(
+            out=xo_s[:].bitcast(I32).rearrange("p (a t q) -> p a t q", t=PACK, q=RUN // 4),
+            in_=xz_s[:].bitcast(I32).rearrange("p (t a q) -> p a t q", t=PACK, q=RUN // 4),
+        )
+        for r in range(TILES):
+            for g in range(G):
+                product(o_bank[r][:, block(g)], r, xo_c, xo_s, block(g), wo_c, wo_s)
+            nc.scalar.copy(out=o_sb[:, r].rearrange("p g n -> p (g n)"), in_=o_bank[r][:])
+
         scale_z(0)
-
-        interleave(nc.vector.tensor_copy, wo_b, wo_raw, 0, HALF)
-        interleave(nc.scalar.copy, ad_b, ad_raw, 0, J)
-        quantize(ad_c[:], ad_s[:], ad_b)
-        quantize(codes_of(wo_q[0]), scales_of(wo_q[0]), wo_b)
-        product(1, x_c, x_s, codes_of(w_q[1]), scales_of(w_q[1]))
-        swap(wo_q)
-        product(0, x_c, x_s, codes_of(wo_q[0]), scales_of(wo_q[0]))
         scale_z(1)
-        copy_o(0)
+        quantize(ad_c[:], ad_s[:], flat(ad_b))
+        quantize_h(0)
+        scale_z(2)
+        quantize_h(1)
+        for c in range(2):
+            for g in range(G - 1):
+                edges(g, c)
+        scale_z(3)
+        quantize_h(2)
+        quantize_h(3)
+        nc.vector.transpose(out=nj_cols[:], in_=nj_rows[:])
+        for c in range(2):
+            edges(G - 1, c)
+        for c in range(2, TILES):
+            for g in range(G):
+                edges(g, c)
 
-        interleave(nc.vector.tensor_copy, h_b[0], h_rows[0], 0, HALF)
-        quantize(h_c[0][:], h_s[0][:], h_b[0])
-        product(1, x_c, x_s, codes_of(wo_q[1]), scales_of(wo_q[1]))
-        product(0, ad_c, ad_s, h_c[0], h_s[0])
-        copy_o(1)
-        combine(0, 0)
-        combine(0, 1)
-        interleave(nc.vector.tensor_copy, h_b[1], h_rows[1], 0, HALF)
-        combine(0, 2)
-        quantize(h_c[1][:], h_s[1][:], h_b[1])
-        product(1, ad_c, ad_s, h_c[1], h_s[1])
-        combine(0, 3)
         for g in range(G):
-            finish(0, g)
-        for g in range(G):
-            combine(1, g)
-            finish(1, g)
+            nc.vector.scalar_tensor_tensor(
+                out=pre[g][:].rearrange("p (r n) -> p r n", r=TILES),
+                in0=zy_bank[g][:].rearrange("p (r n) -> p r n", r=TILES),
+                scalar=nj_cols[:, R * g : R * g + 1],
+                in1=o_sb[:, :, g, :],
+                op0=ALU.mult,
+                op1=ALU.add,
+            )
+            nc.scalar.activation(out=res[g][:], in_=pre[g][:], func=ACT.Relu)
+            nc.sync.dma_start(out=out[g], in_=res[g][:])

@@ -39,6 +39,7 @@ def tile_rows_gnn_sage_kernel(tc, x, w, ni, ad, wo, nj, out):
 
         zy_bank = [ps.tile([P, 512], F32, name=f"zy_bank{r}") for r in range(TILES)]
         o_bank = [ps.tile([P, 512], F32, name=f"o_bank{r}") for r in range(TILES)]
+        y_banks = (zy_bank, o_bank)
 
         x_raw = tile("x_raw", [P, G, PACK, I], F32)
         ad_raw = tile("ad_raw", [P, PACK, J], F32)
@@ -68,14 +69,17 @@ def tile_rows_gnn_sage_kernel(tc, x, w, ni, ad, wo, nj, out):
         h_c = [tile(f"h_c{c}", [P, NT], I32) for c in range(TILES)]
         h_s = [tile(f"h_s{c}", [P, NT], U8) for c in range(TILES)]
         o_sb = tile("o_sb", [P, TILES, G, NT], F32)
-        pre = [tile(f"pre{g}", [P, N], F32) for g in range(G)]
-        res = [tile(f"res{g}", [P, N], F32) for g in range(G)]
+        pre = [[tile(f"pre{u}_{g}", [P, 2, NT], F32) for g in range(G)] for u in range(2)]
+        res = [[tile(f"res{u}_{g}", [P, 2 * NT], F32) for g in range(G)] for u in range(2)]
 
         load_order = (0, 2, 1, 3)
 
-        def load_columns(dst, src):
-            for r in load_order:
-                nc.sync.dma_start(out=dst[rows(r)], in_=src[:, block(r)].rearrange("(p j) n -> p j n", j=PACK))
+        def two_queues(r):
+            return nc.sync if r < 2 else nc.scalar
+
+        def load_columns(dst, src, queue, order):
+            for r in order:
+                queue(r).dma_start(out=dst[rows(r)], in_=src[:, block(r)].rearrange("(p j) n -> p j n", j=PACK))
 
         def interleave(engine_copy, dst, src):
             engine_copy(out=dst[:], in_=src[:].rearrange("p j n -> p n j"))
@@ -115,92 +119,117 @@ def tile_rows_gnn_sage_kernel(tc, x, w, ni, ad, wo, nj, out):
             quantize(h_c[c][:], h_s[c][:], flat(h_b[c]))
 
         def edges(g, c):
-            product(zy_bank[g][:, block(c)], g, ad_c, ad_s, slice(0, J), h_c[c], h_s[c])
+            product(y_banks[c // 2][g][:, block(c % 2)], g, ad_c, ad_s, slice(0, J), h_c[c], h_s[c])
 
-        nc.gpsimd.memset(ni_row[:], 0.0)
-        nc.scalar.dma_start(out=ni_row[0:P:R, :], in_=ni.rearrange("g i o -> g (i o)"))
-        load_columns(w_raw, w)
-        for r in load_order:
-            nc.sync.dma_start(
-                out=x_raw[rows(r)].rearrange("p g j i -> p g (j i)"),
-                in_=x.rearrange("g (p j) i -> p g (j i)", j=PACK),
-            )
-        load_columns(wo_raw, wo)
-        ad_dealt = ad.rearrange("g (b t q) c -> t (g b) q c", t=PACK, q=RUN)
-        for t in range(PACK):
-            nc.sync.dma_start(out=ad_raw[:, t, :], in_=ad_dealt[t])
-
-        nc.gpsimd.memset(nj_rows[:], 0.0)
-        nc.gpsimd.dma_start(
-            out=nj_rows[0:P:R, :].rearrange("q (g a) -> q g a", a=R),
-            in_=nj.rearrange("g (q a) o -> q g (a o)", a=R),
-        )
-        nc.vector.memset(xz_s[:].bitcast(I32), 0)
-
-        interleave(nc.scalar.copy, w_b, w_raw)
-        nc.vector.tensor_copy(
-            out=ni_dealt[:].rearrange("p (t b q) -> p t b q", t=PACK, q=RUN),
-            in_=ni_row[:].rearrange("p (b t q) -> p t b q", t=PACK, q=RUN),
-        )
-        nc.vector.transpose(out=ni_cols[:], in_=ni_dealt[:])
-        nc.vector.tensor_copy(out=ni_t[:], in_=ni_cols[:, 0:P:R])
-        quantize(w_c[:], w_s[:], flat(w_b))
-
-        deal_x(nc.vector.tensor_copy, 0, 0, G)
-        deal_x(nc.scalar.copy, 1, 0, G)
-        deal_x(nc.vector.tensor_copy, 2, 0, G)
-        deal_x(nc.scalar.copy, 3, 2, G)
-        deal_x(nc.vector.tensor_copy, 3, 0, 2)
-        for u in range(2):
-            half = slice(2 * P * u, 2 * P * (u + 1))
-            quantize(xz_c[:, half], xz_s[:, half], x_b[:, 2 * u : 2 * u + 2, :].rearrange("p t e -> p (t e)"))
-        for r in range(TILES):
-            for t in range(PACK):
-                product(zy_bank[r][:, block(t)], r, xz_c, xz_s, block(t), w_c, w_s)
-
-        interleave(nc.scalar.copy, wo_b, wo_raw)
-        interleave(nc.scalar.copy, ad_b, ad_raw)
-        quantize(wo_c[:], wo_s[:], flat(wo_b))
-        nc.vector.tensor_copy(
-            out=xo_c[:].rearrange("p (a t q) -> p a t q", t=PACK, q=RUN),
-            in_=xz_c[:].rearrange("p (t a q) -> p a t q", t=PACK, q=RUN),
-        )
-        nc.vector.tensor_copy(
-            out=xo_s[:].bitcast(I32).rearrange("p (a t q) -> p a t q", t=PACK, q=RUN // 4),
-            in_=xz_s[:].bitcast(I32).rearrange("p (t a q) -> p a t q", t=PACK, q=RUN // 4),
-        )
-        for r in range(TILES):
+        def own_features(r):
             for g in range(G):
                 product(o_bank[r][:, block(g)], r, xo_c, xo_s, block(g), wo_c, wo_s)
             nc.scalar.copy(out=o_sb[:, r].rearrange("p g n -> p (g n)"), in_=o_bank[r][:])
 
-        scale_z(0)
-        scale_z(1)
-        quantize(ad_c[:], ad_s[:], flat(ad_b))
-        quantize_h(0)
-        scale_z(2)
-        quantize_h(1)
-        for c in range(2):
-            for g in range(G - 1):
-                edges(g, c)
-        scale_z(3)
-        quantize_h(2)
-        quantize_h(3)
-        nc.vector.transpose(out=nj_cols[:], in_=nj_rows[:])
-        for c in range(2):
-            edges(G - 1, c)
-        for c in range(2, TILES):
-            for g in range(G):
-                edges(g, c)
-
-        for g in range(G):
+        def combine(u, g):
             nc.vector.scalar_tensor_tensor(
-                out=pre[g][:].rearrange("p (r n) -> p r n", r=TILES),
-                in0=zy_bank[g][:].rearrange("p (r n) -> p r n", r=TILES),
+                out=pre[u][g][:],
+                in0=y_banks[u][g][:, 0 : 2 * NT].rearrange("p (r n) -> p r n", r=2),
                 scalar=nj_cols[:, R * g : R * g + 1],
-                in1=o_sb[:, :, g, :],
+                in1=o_sb[:, 2 * u : 2 * u + 2, g, :],
                 op0=ALU.mult,
                 op1=ALU.add,
             )
-            nc.scalar.activation(out=res[g][:], in_=pre[g][:], func=ACT.Relu)
-            nc.sync.dma_start(out=out[g], in_=res[g][:])
+
+        def finish(u, g, on_vector=False):
+            src = pre[u][g][:].rearrange("p r n -> p (r n)")
+            if on_vector:
+                nc.vector.tensor_scalar_max(out=res[u][g][:], in0=src, scalar1=0.0)
+            else:
+                nc.scalar.activation(out=res[u][g][:], in_=src, func=ACT.Relu)
+            nc.sync.dma_start(out=out[g, :, 2 * NT * u : 2 * NT * (u + 1)], in_=res[u][g][:])
+
+        nc.scalar.dma_start(out=ni_row[0:P:R, :], in_=ni.rearrange("g i o -> g (i o)"))
+        for r in load_order:
+            two_queues(r).dma_start(
+                out=x_raw[rows(r)].rearrange("p g j i -> p g (j i)"),
+                in_=x.rearrange("g (p j) i -> p g (j i)", j=PACK),
+            )
+        load_columns(w_raw, w, lambda r: nc.scalar if r == 2 else nc.sync, load_order)
+        nc.vector.memset(ni_dealt[:], 0.0)
+        nc.scalar.copy(out=nj_rows[:], in_=ni_dealt[:])
+        nc.vector.memset(xz_s[:].bitcast(I32), 0)
+        load_columns(wo_raw, wo, lambda r: nc.sync, load_order)
+        ad_dealt = ad.rearrange("g (b t q) c -> t (g b) q c", t=PACK, q=RUN)
+        for t in range(PACK):
+            nc.sync.dma_start(out=ad_raw[:, t, :], in_=ad_dealt[t])
+
+        nc.sync.dma_start(
+            out=nj_rows[0:P:R, :].rearrange("q (g a) -> q g a", a=R),
+            in_=nj.rearrange("g (q a) o -> q g (a o)", a=R),
+        )
+
+        for g in range(G):
+            nc.vector.tensor_copy(
+                out=ni_dealt[R * g : R * g + 1, :].rearrange("p (t b q) -> p t b q", t=PACK, q=RUN),
+                in_=ni_row[R * g : R * g + 1, :].rearrange("p (b t q) -> p t b q", t=PACK, q=RUN),
+            )
+        nc.vector.transpose(out=ni_cols[:], in_=ni_dealt[:])
+        nc.vector.tensor_copy(out=ni_t[:], in_=ni_cols[:, 0:P:R])
+
+        def quantize_x(u):
+            half = slice(2 * P * u, 2 * P * (u + 1))
+            quantize(xz_c[:, half], xz_s[:, half], x_b[:, 2 * u : 2 * u + 2, :].rearrange("p t e -> p (t e)"))
+
+        deal_x(nc.vector.tensor_copy, 0, 0, G)
+        deal_x(nc.scalar.copy, 1, 0, G)
+        deal_x(nc.vector.tensor_copy, 2, 0, G)
+        deal_x(nc.scalar.copy, 3, 0, G)
+        interleave(nc.vector.tensor_copy, w_b, w_raw)
+        quantize_x(0)
+        quantize(w_c[:], w_s[:], flat(w_b))
+        quantize_x(1)
+        for r in range(TILES):
+            for t in range(PACK):
+                product(zy_bank[r][:, block(t)], r, xz_c, xz_s, block(t), w_c, w_s)
+
+        nc.vector.tensor_copy(
+            out=xo_s[:].bitcast(I32).rearrange("p (a t q) -> p a t q", t=PACK, q=RUN // 4),
+            in_=xz_s[:].bitcast(I32).rearrange("p (t a q) -> p a t q", t=PACK, q=RUN // 4),
+        )
+        nc.vector.tensor_copy(
+            out=xo_c[:].rearrange("p (a t q) -> p a t q", t=PACK, q=RUN),
+            in_=xz_c[:].rearrange("p (t a q) -> p a t q", t=PACK, q=RUN),
+        )
+        interleave(nc.scalar.copy, wo_b, wo_raw)
+        interleave(nc.scalar.copy, ad_b, ad_raw)
+
+        scale_z(0)
+        scale_z(1)
+        quantize(wo_c[:], wo_s[:], flat(wo_b))
+        own_features(0)
+        own_features(1)
+        quantize_h(0)
+        scale_z(2)
+        quantize(ad_c[:], ad_s[:], flat(ad_b))
+        quantize_h(1)
+        for g in range(G - 1):
+            for c in range(2):
+                edges(g, c)
+        own_features(2)
+        own_features(3)
+        scale_z(3)
+        for c in range(2):
+            edges(G - 1, c)
+        nc.vector.transpose(out=nj_cols[:], in_=nj_rows[:])
+        quantize_h(2)
+        combine(0, 0)
+        quantize_h(3)
+        for g in range(G):
+            for c in range(2, TILES):
+                edges(g, c)
+        finish(0, 0)
+        for g in range(1, G):
+            combine(0, g)
+            finish(0, g)
+        for g in range(G):
+            combine(1, g)
+            if g < 2:
+                finish(1, g)
+        for g in range(2, G):
+            finish(1, g, on_vector=True)

@@ -3,7 +3,7 @@ from contextlib import ExitStack
 import concourse.mybir as mybir
 
 G, D, I, N, J = 4, 128, 128, 512, 128
-FLOPS = 3 * 2 * G * 128 * 128 * N
+FLOPS = 2 * G * N * (D * I + I * J + D * J)
 
 F32 = mybir.dt.float32
 BF16 = mybir.dt.bfloat16
@@ -19,6 +19,10 @@ TILES = P // R
 PACK = 4
 RUN = 8
 NT = N // TILES
+BANK = 512
+RECORD = I + I // 4
+SLOTS = G + 1
+RECORD_MOVES = ((0, 1, 2), (2, 1, 2), (0, 2, 2), (2, 0, 2), (0, 3, 1), (2, 3, 1), (1, 0, 1), (3, 0, 1))
 
 
 def tile_rows_gnn_sage_kernel(tc, x, w, ni, ad, wo, nj, out):
@@ -37,11 +41,11 @@ def tile_rows_gnn_sage_kernel(tc, x, w, ni, ad, wo, nj, out):
         def block(c):
             return slice(NT * c, NT * (c + 1))
 
-        zy_bank = [ps.tile([P, 512], F32, name=f"zy_bank{r}") for r in range(TILES)]
-        o_bank = [ps.tile([P, 512], F32, name=f"o_bank{r}") for r in range(TILES)]
-        y_banks = (zy_bank, o_bank)
+        z_bank = [ps.tile([P, BANK], F32, name=f"z_bank{r}") for r in range(TILES)]
+        o_bank = [ps.tile([P, BANK], F32, name=f"o_bank{r}") for r in range(TILES)]
+        y_banks = (z_bank, o_bank)
 
-        x_raw = tile("x_raw", [P, G, PACK, I], F32)
+        x_raw = tile("x_raw", [P, PACK, I], F32)
         ad_raw = tile("ad_raw", [P, PACK, J], F32)
         w_raw = tile("w_raw", [P, PACK, NT], F32)
         wo_raw = tile("wo_raw", [P, PACK, NT], F32)
@@ -50,15 +54,15 @@ def tile_rows_gnn_sage_kernel(tc, x, w, ni, ad, wo, nj, out):
         ni_cols = tile("ni_cols", [P, I], F32)
         nj_rows = tile("nj_rows", [P, J], F32)
         nj_cols = tile("nj_cols", [P, J], F32)
-        ni_t = tile("ni_t", [P, PACK], F32)
-        x_b = tile("x_b", [P, PACK, G * R * PACK], BF16)
+        ni_word = tile("ni_word", [P, PACK], F32)
+        x_b = tile("x_b", [P, I, PACK], BF16)
         ad_b = tile("ad_b", [P, J, PACK], BF16)
         w_b = tile("w_b", [P, NT, PACK], BF16)
         wo_b = tile("wo_b", [P, NT, PACK], BF16)
-        xz_c = tile("xz_c", [P, G * I], I32)
-        xz_s = tile("xz_s", [P, G * I], U8)
-        xo_c = tile("xo_c", [P, G * I], I32)
-        xo_s = tile("xo_s", [P, G * I], U8)
+        x_own = tile("x_own", [P, RECORD], I32)
+        x_all = tile("x_all", [P, SLOTS, RECORD], I32)
+        xz_c = tile("xz_c", [P, PACK, SLOTS * R], I32)
+        xz_s = [tile(f"xz_s{first}", [P, PACK, G * R], U8) for first in range(2)]
         w_c = tile("w_c", [P, NT], I32)
         w_s = tile("w_s", [P, NT], U8)
         wo_c = tile("wo_c", [P, NT], I32)
@@ -69,167 +73,169 @@ def tile_rows_gnn_sage_kernel(tc, x, w, ni, ad, wo, nj, out):
         h_c = [tile(f"h_c{c}", [P, NT], I32) for c in range(TILES)]
         h_s = [tile(f"h_s{c}", [P, NT], U8) for c in range(TILES)]
         o_sb = tile("o_sb", [P, TILES, G, NT], F32)
-        pre = [[tile(f"pre{u}_{g}", [P, 2, NT], F32) for g in range(G)] for u in range(2)]
-        res = [[tile(f"res{u}_{g}", [P, 2 * NT], F32) for g in range(G)] for u in range(2)]
+        pre = [[tile(f"pre{half}_{g}", [P, 2, NT], F32) for g in range(G)] for half in range(2)]
+        res = [[tile(f"res{half}_{g}", [P, 2 * NT], F32) for g in range(G)] for half in range(2)]
 
-        load_order = (0, 2, 1, 3)
+        def load_columns(dst, src, tiles):
+            for r in tiles:
+                nc.sync.dma_start(out=dst[rows(r)], in_=src[:, block(r)].rearrange("(p t) n -> p t n", t=PACK))
 
-        def two_queues(r):
-            return nc.sync if r < 2 else nc.scalar
+        def first_slot(r):
+            return 1 - r % 2
 
-        def load_columns(dst, src, queue, order):
-            for r in order:
-                queue(r).dma_start(out=dst[rows(r)], in_=src[:, block(r)].rearrange("(p j) n -> p j n", j=PACK))
+        def scales_of(record):
+            return record[:, I:RECORD].bitcast(U8)
 
         def interleave(engine_copy, dst, src):
-            engine_copy(out=dst[:], in_=src[:].rearrange("p j n -> p n j"))
-
-        def deal_x(engine_copy, t, g0, g1):
-            engine_copy(
-                out=x_b[:, t, g0 * R * PACK : g1 * R * PACK].rearrange("p (g b q j) -> p g b q j", b=4, q=RUN, j=PACK),
-                in_=x_raw[:, g0:g1].rearrange("p g j (b t q) -> p t g b q j", t=PACK, q=RUN)[:, t],
-            )
+            engine_copy(out=dst, in_=src.rearrange("p t n -> p n t"))
 
         def quantize(codes, scales, src):
-            nc.vector.quantize_mx(out=codes.bitcast(FP8X4), scales=scales, in_=src)
+            nc.vector.quantize_mx(out=codes.bitcast(FP8X4), scales=scales, in_=src.rearrange("p n t -> p (n t)"))
 
-        def flat(t):
-            return t[:].rearrange("p n j -> p (n j)")
-
-        def product(dst, r, lhs_c, lhs_s, m, rhs_c, rhs_s):
+        def product(dst, r, lhs_c, lhs_s, rhs_c, rhs_s):
             nc.tensor.matmul_mx(
                 out=dst,
-                lhsT=lhs_c[rows(r), m].bitcast(FP8X4),
-                lhsT_scale=lhs_s[rows(r), m],
+                lhsT=lhs_c[rows(r), :].bitcast(FP8X4),
+                lhsT_scale=lhs_s[rows(r), :],
                 rhs=rhs_c[rows(r), :].bitcast(FP8X4),
                 rhs_scale=rhs_s[rows(r), :],
                 start=True,
                 stop=True,
             )
 
+        def deal_x_scales(first):
+            nc.vector.tensor_copy(
+                out=xz_s[first][:].bitcast(I32).rearrange("p t (g b q) -> p t g b q", g=G, q=RUN // 4),
+                in_=x_all[:, first : first + G, I:RECORD].rearrange("p g (b t q) -> p t g b q", t=PACK, q=RUN // 4),
+            )
+
+        def deal_x_codes(places):
+            nc.vector.tensor_copy(
+                out=xz_c[:, places, :].rearrange("p t (s b q) -> p t s b q", s=SLOTS, q=RUN),
+                in_=x_all[:, :, 0:I].rearrange("p s (b t q) -> p t s b q", t=PACK, q=RUN)[:, places],
+            )
+
         def scale_z(c):
             nc.vector.tensor_tensor(
                 out=h_b[c][:],
-                in0=zy_bank[c][:].rearrange("p (t n) -> p n t", t=PACK),
-                in1=ni_t[:].unsqueeze(1).to_broadcast([P, NT, PACK]),
+                in0=z_bank[c][:].rearrange("p (t n) -> p n t", t=PACK),
+                in1=ni_word[:].unsqueeze(1).to_broadcast([P, NT, PACK]),
                 op=ALU.mult,
             )
 
         def quantize_h(c):
-            quantize(h_c[c][:], h_s[c][:], flat(h_b[c]))
+            quantize(h_c[c][:], h_s[c][:], h_b[c][:])
 
-        def edges(g, c):
-            product(y_banks[c // 2][g][:, block(c % 2)], g, ad_c, ad_s, slice(0, J), h_c[c], h_s[c])
+        def edges(half):
+            for g in range(G):
+                for k in range(2):
+                    c = 2 * half + k
+                    product(y_banks[half][g][:, block(k)], g, ad_c, ad_s, h_c[c], h_s[c])
 
         def own_features(r):
             for g in range(G):
-                product(o_bank[r][:, block(g)], r, xo_c, xo_s, block(g), wo_c, wo_s)
+                record = x_all[:, first_slot(r) + g, :]
+                product(o_bank[r][:, block(g)], r, record[:, 0:I], scales_of(record), wo_c, wo_s)
             nc.scalar.copy(out=o_sb[:, r].rearrange("p g n -> p (g n)"), in_=o_bank[r][:])
 
-        def combine(u, g):
+        def combine(half, g):
             nc.vector.scalar_tensor_tensor(
-                out=pre[u][g][:],
-                in0=y_banks[u][g][:, 0 : 2 * NT].rearrange("p (r n) -> p r n", r=2),
+                out=pre[half][g][:],
+                in0=y_banks[half][g][:, 0 : 2 * NT].rearrange("p (k n) -> p k n", k=2),
                 scalar=nj_cols[:, R * g : R * g + 1],
-                in1=o_sb[:, 2 * u : 2 * u + 2, g, :],
+                in1=o_sb[:, 2 * half : 2 * half + 2, g, :],
                 op0=ALU.mult,
                 op1=ALU.add,
             )
 
-        def finish(u, g, on_vector=False):
-            src = pre[u][g][:].rearrange("p r n -> p (r n)")
+        def finish(half, g, on_vector=False):
+            src = pre[half][g][:].rearrange("p k n -> p (k n)")
             if on_vector:
-                nc.vector.tensor_scalar_max(out=res[u][g][:], in0=src, scalar1=0.0)
+                nc.vector.tensor_scalar_max(out=res[half][g][:], in0=src, scalar1=0.0)
             else:
-                nc.scalar.activation(out=res[u][g][:], in_=src, func=ACT.Relu)
-            nc.sync.dma_start(out=out[g, :, 2 * NT * u : 2 * NT * (u + 1)], in_=res[u][g][:])
+                nc.scalar.activation(out=res[half][g][:], in_=src, func=ACT.Relu)
+            nc.sync.dma_start(out=out[g, :, 2 * NT * half : 2 * NT * (half + 1)], in_=res[half][g][:])
 
         nc.scalar.dma_start(out=ni_row[0:P:R, :], in_=ni.rearrange("g i o -> g (i o)"))
-        for r in load_order:
-            two_queues(r).dma_start(
-                out=x_raw[rows(r)].rearrange("p g j i -> p g (j i)"),
-                in_=x.rearrange("g (p j) i -> p g (j i)", j=PACK),
-            )
-        load_columns(w_raw, w, lambda r: nc.scalar if r == 2 else nc.sync, load_order)
+        nc.sync.dma_start(out=x_raw[:], in_=x.rearrange("g (p t) i -> (g p) t i", t=PACK))
+        load_columns(w_raw, w, (0, 2, 1, 3))
+        load_columns(wo_raw, wo, (0, 2))
+
         nc.vector.memset(ni_dealt[:], 0.0)
         nc.scalar.copy(out=nj_rows[:], in_=ni_dealt[:])
-        nc.vector.memset(xz_s[:].bitcast(I32), 0)
-        load_columns(wo_raw, wo, lambda r: nc.sync, load_order)
-        ad_dealt = ad.rearrange("g (b t q) c -> t (g b) q c", t=PACK, q=RUN)
+        nc.vector.memset(x_own[:, I:RECORD], 0)
+        nc.vector.memset(x_all[:, 0:SLOTS:G, :], 0)
+
+        node_halves = (slice(0, I // 2), slice(I // 2, I))
+        for nodes in node_halves:
+            interleave(nc.vector.tensor_copy, x_b[:, nodes, :], x_raw[:, :, nodes])
+        for nodes in node_halves:
+            quantize(x_own[:, nodes], scales_of(x_own)[:, nodes], x_b[:, nodes, :])
+
+        for r0, g0, count in RECORD_MOVES:
+            nc.sync.dma_start(
+                out=x_all[R * r0 : R * (r0 + count), first_slot(r0) + g0, :],
+                in_=x_own[R * g0 : R * (g0 + count), :],
+            )
+        load_columns(wo_raw, wo, (1, 3))
+        ad_dealt = ad.rearrange("g (b t q) j -> t (g b) q j", t=PACK, q=RUN)
         for t in range(PACK):
             nc.sync.dma_start(out=ad_raw[:, t, :], in_=ad_dealt[t])
-
         nc.sync.dma_start(
-            out=nj_rows[0:P:R, :].rearrange("q (g a) -> q g a", a=R),
-            in_=nj.rearrange("g (q a) o -> q g (a o)", a=R),
+            out=nj_rows[0:P:R, :].rearrange("r (g a) -> r g a", a=R),
+            in_=nj.rearrange("g (r a) o -> r g (a o)", a=R),
         )
 
+        for r0 in (0, 2):
+            pair = slice(R * r0, R * (r0 + 2))
+            nc.vector.tensor_copy(out=x_all[pair, first_slot(r0) + r0, :], in_=x_own[pair, :])
         for g in range(G):
             nc.vector.tensor_copy(
                 out=ni_dealt[R * g : R * g + 1, :].rearrange("p (t b q) -> p t b q", t=PACK, q=RUN),
                 in_=ni_row[R * g : R * g + 1, :].rearrange("p (b t q) -> p t b q", t=PACK, q=RUN),
             )
+        interleave(nc.vector.tensor_copy, w_b[:], w_raw[:])
         nc.vector.transpose(out=ni_cols[:], in_=ni_dealt[:])
-        nc.vector.tensor_copy(out=ni_t[:], in_=ni_cols[:, 0:P:R])
+        quantize(w_c[:], w_s[:], w_b[:])
+        nc.vector.tensor_copy(out=ni_word[:], in_=ni_cols[:, 0:P:R])
 
-        def quantize_x(u):
-            half = slice(2 * P * u, 2 * P * (u + 1))
-            quantize(xz_c[:, half], xz_s[:, half], x_b[:, 2 * u : 2 * u + 2, :].rearrange("p t e -> p (t e)"))
-
-        deal_x(nc.vector.tensor_copy, 0, 0, G)
-        deal_x(nc.scalar.copy, 1, 0, G)
-        deal_x(nc.vector.tensor_copy, 2, 0, G)
-        deal_x(nc.scalar.copy, 3, 0, G)
-        interleave(nc.vector.tensor_copy, w_b, w_raw)
-        quantize_x(0)
-        quantize(w_c[:], w_s[:], flat(w_b))
-        quantize_x(1)
+        deal_x_scales(first_slot(0))
+        deal_x_codes(slice(0, 2))
+        deal_x_codes(slice(2, 4))
+        deal_x_scales(first_slot(1))
         for r in range(TILES):
+            first = first_slot(r)
             for t in range(PACK):
-                product(zy_bank[r][:, block(t)], r, xz_c, xz_s, block(t), w_c, w_s)
+                graphs = slice(R * first, R * (first + G))
+                product(z_bank[r][:, block(t)], r, xz_c[:, t, graphs], xz_s[first][:, t, :], w_c, w_s)
 
-        nc.vector.tensor_copy(
-            out=xo_s[:].bitcast(I32).rearrange("p (a t q) -> p a t q", t=PACK, q=RUN // 4),
-            in_=xz_s[:].bitcast(I32).rearrange("p (t a q) -> p a t q", t=PACK, q=RUN // 4),
-        )
-        nc.vector.tensor_copy(
-            out=xo_c[:].rearrange("p (a t q) -> p a t q", t=PACK, q=RUN),
-            in_=xz_c[:].rearrange("p (t a q) -> p a t q", t=PACK, q=RUN),
-        )
-        interleave(nc.scalar.copy, wo_b, wo_raw)
-        interleave(nc.scalar.copy, ad_b, ad_raw)
+        interleave(nc.scalar.copy, wo_b[:], wo_raw[:])
+        interleave(nc.scalar.copy, ad_b[:], ad_raw[:])
 
         scale_z(0)
         scale_z(1)
-        quantize(wo_c[:], wo_s[:], flat(wo_b))
-        own_features(0)
-        own_features(1)
         quantize_h(0)
+        quantize(wo_c[:], wo_s[:], wo_b[:])
+        for r in range(TILES):
+            own_features(r)
         scale_z(2)
-        quantize(ad_c[:], ad_s[:], flat(ad_b))
         quantize_h(1)
-        for g in range(G - 1):
-            for c in range(2):
-                edges(g, c)
-        own_features(2)
-        own_features(3)
         scale_z(3)
-        for c in range(2):
-            edges(G - 1, c)
+        quantize(ad_c[:], ad_s[:], ad_b[:])
+        edges(0)
         nc.vector.transpose(out=nj_cols[:], in_=nj_rows[:])
         quantize_h(2)
         combine(0, 0)
         quantize_h(3)
-        for g in range(G):
-            for c in range(2, TILES):
-                edges(g, c)
+        edges(1)
         finish(0, 0)
         for g in range(1, G):
             combine(0, g)
             finish(0, g)
+        on_scalar = 2
         for g in range(G):
             combine(1, g)
-            if g < 2:
+            if g < on_scalar:
                 finish(1, g)
-        for g in range(2, G):
+        for g in range(on_scalar, G):
             finish(1, g, on_vector=True)

from contextlib import ExitStack

import concourse.mybir as mybir

G, D, I, N, J = 4, 128, 128, 512, 128
FLOPS = 2 * G * N * (D * I + I * J + D * J)

F32 = mybir.dt.float32
BF16 = mybir.dt.bfloat16
I32 = mybir.dt.int32
U8 = mybir.dt.uint8
FP8X4 = mybir.dt.float8_e4m3fn_x4
ACT = mybir.ActivationFunctionType
ALU = mybir.AluOpType

P = 128
R = 32
TILES = P // R
PACK = 4
RUN = 8
NT = N // TILES
BANK = 512
RECORD = I + I // 4
SLOTS = G + 1
RECORD_MOVES = ((0, 1, 2), (2, 1, 2), (0, 2, 2), (2, 0, 2), (0, 3, 1), (2, 3, 1), (1, 0, 1), (3, 0, 1))


def tile_rows_gnn_sage_kernel(tc, x, w, ni, ad, wo, nj, out):
    nc = tc.nc
    with ExitStack() as ctx:
        sb = ctx.enter_context(tc.tile_pool(name="sb", bufs=1))
        ps = ctx.enter_context(tc.psum_pool(name="ps", bufs=1))
        ctx.enter_context(tc.manual_schedule())

        def tile(name, shape, dtype):
            return sb.tile(shape, dtype, name=name, align_bytes=64)

        def rows(r):
            return slice(R * r, R * (r + 1))

        def block(c):
            return slice(NT * c, NT * (c + 1))

        z_bank = [ps.tile([P, BANK], F32, name=f"z_bank{r}") for r in range(TILES)]
        o_bank = [ps.tile([P, BANK], F32, name=f"o_bank{r}") for r in range(TILES)]
        y_banks = (z_bank, o_bank)

        x_raw = tile("x_raw", [P, PACK, I], F32)
        ad_raw = tile("ad_raw", [P, PACK, J], F32)
        w_raw = tile("w_raw", [P, PACK, NT], F32)
        wo_raw = tile("wo_raw", [P, PACK, NT], F32)
        ni_row = tile("ni_row", [P, I], F32)
        ni_dealt = tile("ni_dealt", [P, I], F32)
        ni_cols = tile("ni_cols", [P, I], F32)
        nj_rows = tile("nj_rows", [P, J], F32)
        nj_cols = tile("nj_cols", [P, J], F32)
        ni_word = tile("ni_word", [P, PACK], F32)
        x_b = tile("x_b", [P, I, PACK], BF16)
        ad_b = tile("ad_b", [P, J, PACK], BF16)
        w_b = tile("w_b", [P, NT, PACK], BF16)
        wo_b = tile("wo_b", [P, NT, PACK], BF16)
        x_own = tile("x_own", [P, RECORD], I32)
        x_all = tile("x_all", [P, SLOTS, RECORD], I32)
        xz_c = tile("xz_c", [P, PACK, SLOTS * R], I32)
        xz_s = [tile(f"xz_s{first}", [P, PACK, G * R], U8) for first in range(2)]
        w_c = tile("w_c", [P, NT], I32)
        w_s = tile("w_s", [P, NT], U8)
        wo_c = tile("wo_c", [P, NT], I32)
        wo_s = tile("wo_s", [P, NT], U8)
        ad_c = tile("ad_c", [P, J], I32)
        ad_s = tile("ad_s", [P, J], U8)
        h_b = [tile(f"h_b{c}", [P, NT, PACK], BF16) for c in range(TILES)]
        h_c = [tile(f"h_c{c}", [P, NT], I32) for c in range(TILES)]
        h_s = [tile(f"h_s{c}", [P, NT], U8) for c in range(TILES)]
        o_sb = tile("o_sb", [P, TILES, G, NT], F32)
        pre = [[tile(f"pre{half}_{g}", [P, 2, NT], F32) for g in range(G)] for half in range(2)]
        res = [[tile(f"res{half}_{g}", [P, 2 * NT], F32) for g in range(G)] for half in range(2)]

        def load_columns(dst, src, tiles):
            for r in tiles:
                nc.sync.dma_start(out=dst[rows(r)], in_=src[:, block(r)].rearrange("(p t) n -> p t n", t=PACK))

        def first_slot(r):
            return 1 - r % 2

        def scales_of(record):
            return record[:, I:RECORD].bitcast(U8)

        def interleave(engine_copy, dst, src):
            engine_copy(out=dst, in_=src.rearrange("p t n -> p n t"))

        def quantize(codes, scales, src):
            nc.vector.quantize_mx(out=codes.bitcast(FP8X4), scales=scales, in_=src.rearrange("p n t -> p (n t)"))

        def product(dst, r, lhs_c, lhs_s, rhs_c, rhs_s):
            nc.tensor.matmul_mx(
                out=dst,
                lhsT=lhs_c[rows(r), :].bitcast(FP8X4),
                lhsT_scale=lhs_s[rows(r), :],
                rhs=rhs_c[rows(r), :].bitcast(FP8X4),
                rhs_scale=rhs_s[rows(r), :],
                start=True,
                stop=True,
            )

        def deal_x_scales(first):
            nc.vector.tensor_copy(
                out=xz_s[first][:].bitcast(I32).rearrange("p t (g b q) -> p t g b q", g=G, q=RUN // 4),
                in_=x_all[:, first : first + G, I:RECORD].rearrange("p g (b t q) -> p t g b q", t=PACK, q=RUN // 4),
            )

        def deal_x_codes(places):
            nc.vector.tensor_copy(
                out=xz_c[:, places, :].rearrange("p t (s b q) -> p t s b q", s=SLOTS, q=RUN),
                in_=x_all[:, :, 0:I].rearrange("p s (b t q) -> p t s b q", t=PACK, q=RUN)[:, places],
            )

        def scale_z(c):
            nc.vector.tensor_tensor(
                out=h_b[c][:],
                in0=z_bank[c][:].rearrange("p (t n) -> p n t", t=PACK),
                in1=ni_word[:].unsqueeze(1).to_broadcast([P, NT, PACK]),
                op=ALU.mult,
            )

        def quantize_h(c):
            quantize(h_c[c][:], h_s[c][:], h_b[c][:])

        def edges(half):
            for g in range(G):
                for k in range(2):
                    c = 2 * half + k
                    product(y_banks[half][g][:, block(k)], g, ad_c, ad_s, h_c[c], h_s[c])

        def own_features(r):
            for g in range(G):
                record = x_all[:, first_slot(r) + g, :]
                product(o_bank[r][:, block(g)], r, record[:, 0:I], scales_of(record), wo_c, wo_s)
            nc.scalar.copy(out=o_sb[:, r].rearrange("p g n -> p (g n)"), in_=o_bank[r][:])

        def combine(half, g):
            nc.vector.scalar_tensor_tensor(
                out=pre[half][g][:],
                in0=y_banks[half][g][:, 0 : 2 * NT].rearrange("p (k n) -> p k n", k=2),
                scalar=nj_cols[:, R * g : R * g + 1],
                in1=o_sb[:, 2 * half : 2 * half + 2, g, :],
                op0=ALU.mult,
                op1=ALU.add,
            )

        def finish(half, g, on_vector=False):
            src = pre[half][g][:].rearrange("p k n -> p (k n)")
            if on_vector:
                nc.vector.tensor_scalar_max(out=res[half][g][:], in0=src, scalar1=0.0)
            else:
                nc.scalar.activation(out=res[half][g][:], in_=src, func=ACT.Relu)
            nc.sync.dma_start(out=out[g, :, 2 * NT * half : 2 * NT * (half + 1)], in_=res[half][g][:])

        nc.scalar.dma_start(out=ni_row[0:P:R, :], in_=ni.rearrange("g i o -> g (i o)"))
        nc.sync.dma_start(out=x_raw[:], in_=x.rearrange("g (p t) i -> (g p) t i", t=PACK))
        load_columns(w_raw, w, (0, 2, 1, 3))
        load_columns(wo_raw, wo, (0, 2))

        nc.vector.memset(ni_dealt[:], 0.0)
        nc.scalar.copy(out=nj_rows[:], in_=ni_dealt[:])
        nc.vector.memset(x_own[:, I:RECORD], 0)
        nc.vector.memset(x_all[:, 0:SLOTS:G, :], 0)

        node_halves = (slice(0, I // 2), slice(I // 2, I))
        for nodes in node_halves:
            interleave(nc.vector.tensor_copy, x_b[:, nodes, :], x_raw[:, :, nodes])
        for nodes in node_halves:
            quantize(x_own[:, nodes], scales_of(x_own)[:, nodes], x_b[:, nodes, :])

        for r0, g0, count in RECORD_MOVES:
            nc.sync.dma_start(
                out=x_all[R * r0 : R * (r0 + count), first_slot(r0) + g0, :],
                in_=x_own[R * g0 : R * (g0 + count), :],
            )
        load_columns(wo_raw, wo, (1, 3))
        ad_dealt = ad.rearrange("g (b t q) j -> t (g b) q j", t=PACK, q=RUN)
        for t in range(PACK):
            nc.sync.dma_start(out=ad_raw[:, t, :], in_=ad_dealt[t])
        nc.sync.dma_start(
            out=nj_rows[0:P:R, :].rearrange("r (g a) -> r g a", a=R),
            in_=nj.rearrange("g (r a) o -> r g (a o)", a=R),
        )

        for r0 in (0, 2):
            pair = slice(R * r0, R * (r0 + 2))
            nc.vector.tensor_copy(out=x_all[pair, first_slot(r0) + r0, :], in_=x_own[pair, :])
        for g in range(G):
            nc.vector.tensor_copy(
                out=ni_dealt[R * g : R * g + 1, :].rearrange("p (t b q) -> p t b q", t=PACK, q=RUN),
                in_=ni_row[R * g : R * g + 1, :].rearrange("p (b t q) -> p t b q", t=PACK, q=RUN),
            )
        interleave(nc.vector.tensor_copy, w_b[:], w_raw[:])
        nc.vector.transpose(out=ni_cols[:], in_=ni_dealt[:])
        quantize(w_c[:], w_s[:], w_b[:])
        nc.vector.tensor_copy(out=ni_word[:], in_=ni_cols[:, 0:P:R])

        deal_x_scales(first_slot(0))
        deal_x_codes(slice(0, 2))
        deal_x_codes(slice(2, 4))
        deal_x_scales(first_slot(1))
        for r in range(TILES):
            first = first_slot(r)
            for t in range(PACK):
                graphs = slice(R * first, R * (first + G))
                product(z_bank[r][:, block(t)], r, xz_c[:, t, graphs], xz_s[first][:, t, :], w_c, w_s)

        interleave(nc.scalar.copy, wo_b[:], wo_raw[:])
        interleave(nc.scalar.copy, ad_b[:], ad_raw[:])

        scale_z(0)
        scale_z(1)
        quantize_h(0)
        quantize(wo_c[:], wo_s[:], wo_b[:])
        for r in range(TILES):
            own_features(r)
        scale_z(2)
        quantize_h(1)
        scale_z(3)
        quantize(ad_c[:], ad_s[:], ad_b[:])
        edges(0)
        nc.vector.transpose(out=nj_cols[:], in_=nj_rows[:])
        quantize_h(2)
        combine(0, 0)
        quantize_h(3)
        edges(1)
        finish(0, 0)
        for g in range(1, G):
            combine(0, g)
            finish(0, g)
        on_scalar = 2
        for g in range(G):
            combine(1, g)
            if g < on_scalar:
                finish(1, g)
        for g in range(on_scalar, G):
            finish(1, g, on_vector=True)
